import numpy as np
import ml_dtypes


def mxq(x, axis, fmt="e4m3"):
    dtype, down = {"e4m3": (ml_dtypes.float8_e4m3fn, 7), "e5m2": (ml_dtypes.float8_e5m2, 14)}[fmt]
    v = np.moveaxis(np.asarray(x, np.float32).astype(ml_dtypes.bfloat16).astype(np.float64), axis, -1)
    blocks = v.reshape(v.shape[:-1] + (-1, 32))
    amax = np.abs(blocks).max(-1, keepdims=True)
    byte = np.maximum(np.where(amax > 0, np.frexp(amax)[1] - 1 + 127, 0) - down, 1)
    scale = np.exp2(byte - 127.0)
    codes = (blocks / scale).astype(np.float32).astype(dtype).astype(np.float64)
    return np.moveaxis((codes * scale).reshape(v.shape), -1, axis)


WIDE = False


def mx_kscale(k):
    if not WIDE:
        return np.ones(k)
    levels = np.array([10, -10, 5, -5, 0])
    if k % 512:
        return np.exp2(np.random.permutation(np.resize(levels, k // 32))).repeat(32)
    a = np.empty((k // 512, 16))
    for p in range(k // 512):
        a[p, :8] = np.random.permutation(np.resize(levels, 8))
        for g in range(8):
            far = levels[np.abs(levels - a[p, g]) >= 10]
            a[p, g + 8] = far[np.random.randint(len(far))]
    return np.exp2(a.ravel()).repeat(32)


def f64(x):
    return np.asarray(x).astype(np.float64)


def striped(idx):
    return np.tile(idx.reshape(-1, 16).T, (8, 1)).astype(np.uint16)


def unstriped(offs):
    return offs[:16].T.reshape(-1).astype(np.int64)


def striped8(idx):
    return np.concatenate([x.reshape(-1, 16).T for x in idx]).astype(np.uint16)


def runs(offs, k):
    lists = np.stack([offs[16 * r : 16 * r + 16].T.reshape(-1) for r in range(8)]).astype(np.int64)
    return lists[np.arange(k) % 512 // 64]


def pack_weight(w):
    k, n = w.shape
    w = f64(np.asarray(w, np.float32).astype(ml_dtypes.bfloat16)).reshape(k // 32, 32, n)
    amax = np.abs(w).max(1)
    byte = np.clip(np.where(amax > 0, np.frexp(amax)[1] - 1 + 127 - 7, 1), 1, 254)
    scaled = (w * np.exp2(127.0 - byte)[:, None, :]).reshape(k, n).astype(np.float32)
    words = np.ascontiguousarray(scaled.reshape(k // 512, 128, 4, n).transpose(0, 1, 3, 2)).astype(ml_dtypes.float8_e4m3fn).view(np.uint8)
    return words, np.ascontiguousarray(byte.astype(np.uint8).reshape(k // 512, 16, n))


def unpack_weight(words, scales):
    g, p, n, _ = words.shape
    vals = np.ascontiguousarray(words).view(ml_dtypes.float8_e4m3fn).astype(np.float64) * np.repeat(np.exp2(scales.astype(np.float64) - 127.0), 8, axis=1)[..., None]
    return vals.transpose(0, 1, 3, 2).reshape(g * 512, n)


def sigmoid(v):
    return 1.0 / (1.0 + np.exp(-np.maximum(v, -700.0)))

def planes(y):
    n, m = y.shape
    v = y.astype(np.float32).astype(ml_dtypes.bfloat16).astype(np.float64).reshape(n // 32, 32, m)
    top = np.abs(v).max(1)
    byte = np.clip(np.where(top > 0, np.frexp(top)[1] - 1 + 127 - 7, 1), 1, 254)
    codes = (v * np.exp2(127.0 - byte)[:, None, :]).reshape(n, m).astype(np.float32).astype(ml_dtypes.float8_e4m3fn).view(np.uint8)
    words = codes.reshape(n // 512, 128, 4, m).transpose(0, 1, 3, 2)
    return np.ascontiguousarray(words), np.ascontiguousarray(byte.astype(np.uint8).reshape(n // 512, 16, m))


K, T, S, G, H, C, W = 512, 1024, 256, 2048, 512, 512, 128


def setup_inputs():
    n = np.random.standard_normal
    s = mx_kscale(K)[:, None]
    packed_xT = pack_weight(n((K, T)) * s)
    packed_dT = pack_weight(n((K, G)) / s)
    perm = np.random.permutation(S)
    return {
        "x_words": packed_xT[0],
        "x_scales": packed_xT[1],
        "d_words": packed_dT[0],
        "d_scales": packed_dT[1],
        "sl": np.random.uniform(1.0, 2.0, (H, 1)).astype(np.float32),
        "th": (0.5 * n((H, 1))).astype(np.float32),
        "gs": (np.random.uniform(0.5, 1.5, (K, 1)) / s).astype(np.float32),
        "offs": striped(np.random.permutation(T)[:S]),
        "k1": striped8(np.random.randint(0, G, (8, H))),
        "n1": striped(np.random.permutation(S)),
        "n2": striped(np.random.permutation(S)),
        "cand": striped8(np.random.randint(0, T, (8, C))),
        "n3": striped(perm[:W]),
        "n4": striped(perm[W:]),
        "n5": striped(np.random.permutation(S)),
    }


def reference(x_words, x_scales, d_words, d_scales, sl, th, gs, offs, k1, n1, n2, cand, n3, n4, n5):
    x_cand = unpack_weight(x_words, x_scales)[np.arange(K)[:, None], runs(cand, K)]
    d_k1 = unpack_weight(d_words, d_scales)[np.arange(K)[:, None], runs(k1, K)]
    xq = unpack_weight(x_words, x_scales)[:, unstriped(offs)]
    h = 0.0625 * (d_k1.T @ xq)
    ds = np.zeros((H, S))
    ds[:, unstriped(n1)] = h
    sg = sigmoid(f64(sl) * (ds[:, unstriped(n2)] - f64(th)))
    z = f64(gs) * (h * sg)
    s = 0.0625 * ((x_cand.T @ mxq(z, 0, "e4m3")))
    pa = s[:, unstriped(n3)]
    pb = s[:, unstriped(n4)]
    rb = pa - pb
    ds2 = np.zeros((C, S))
    ds2[:, unstriped(n3)] = pb
    dt = ds2.copy()
    dt[:, unstriped(n4)] = rb
    out_0 = np.maximum(dt, 0.5 * dt[:, unstriped(n5)])
    return (out_0,) + planes(out_0)

@@ -1,0 +1,200 @@
+from contextlib import ExitStack
+
+import concourse.mybir as mybir
+
+K, T, S, G, H, C, W = 512, 1024, 256, 2048, 512, 512, 128
+FLOPS = 2 * K * H * S + 2 * K * C * S
+
+F32 = mybir.dt.float32
+BF16 = mybir.dt.bfloat16
+I32 = mybir.dt.int32
+U32 = mybir.dt.uint32
+U16 = mybir.dt.uint16
+U8 = mybir.dt.uint8
+FP8X4 = mybir.dt.float8_e4m3fn_x4
+ACT = mybir.ActivationFunctionType
+ALU = mybir.AluOpType
+
+P = 128
+PACK = 4
+HALF = S // 2
+PER_COL = 16
+
+
+def tile_picked_pqhcerlswapd_none_po_kernel(
+    tc, x_words, x_scales, d_words, d_scales, sl, th, gs, offs, k1, n1, n2, cand, n3, n4, n5, out_0, out_1, out_2
+):
+    nc = tc.nc
+    tiles = range(PACK)
+    halves = range(2)
+
+    def cols(half):
+        return slice(half * HALF, (half + 1) * HALF)
+
+    def entries(half):
+        return slice(half * HALF // PER_COL, (half + 1) * HALF // PER_COL)
+
+    with ExitStack() as ctx:
+        keep = ctx.enter_context(tc.tile_pool(name="keep", bufs=1))
+        psum = ctx.enter_context(tc.psum_pool(name="psum", bufs=1))
+
+        def new(shape, dtype, name, over=None):
+            return keep.tile(shape, dtype, name=name, tag=over or name, align_bytes=64)
+
+        def load_list(src, name):
+            lst = new(list(src.shape), U16, name)
+            nc.sync.dma_start(lst[:], src)
+            return lst
+
+        def zeroed_bytes(engine, width, name):
+            plane = new([P, width], U8, name)
+            engine.memset(plane[:].bitcast(I32), 0)
+            return plane
+
+        def load_words(queue, src, name):
+            words = new([P, src.shape[2]], U32, name)
+            queue.dma_start(words[:].bitcast(I32), src[0].rearrange("p n t -> p (n t)").bitcast(I32))
+            return words
+
+        def load_scale_rows(win, src):
+            rows = src[0].bitcast(I32)
+            nc.sync.dma_start(win[:].bitcast(I32), rows.unsqueeze(1).to_broadcast([16, 8, rows.shape[1]]))
+
+        def place_scale_rows(queues, picked, placed):
+            for r in range(4):
+                queues[r % len(queues)].dma_start(
+                    placed[r:P:32, :].bitcast(I32), picked[8 * r : P : 32, :].bitcast(I32)
+                )
+
+        def deal(src, dtype, t, name):
+            dealt = new([P, P], dtype, name)
+            nc.vector.tensor_copy(dealt[:], src[:, :H].rearrange("p (m t) -> p t m", t=PACK)[:, t, :])
+            return dealt
+
+        d_sc_win = new([P, G], U8, "d_sc_win")
+        x_sc_win = new([P, T], U8, "x_sc_win")
+        sc_placed = zeroed_bytes(nc.vector, H + S, "sc_placed")
+        c_sc_placed = zeroed_bytes(nc.vector, C, "c_sc_placed")
+
+        k1_l = load_list(k1, "k1_l")
+        d_win = load_words(nc.scalar, d_words, "d_win")
+        offs_l = load_list(offs, "offs_l")
+        x_win = load_words(nc.scalar, x_words, "x_win")
+        load_scale_rows(x_sc_win, x_scales)
+        load_scale_rows(d_sc_win, d_scales)
+        n1_l = load_list(n1, "n1_l")
+        n2_l = load_list(n2, "n2_l")
+        cand_l = load_list(cand, "cand_l")
+        n3_l = load_list(n3, "n3_l")
+        n4_l = load_list(n4, "n4_l")
+        n5_l = load_list(n5, "n5_l")
+
+        row_vals = []
+        for src, name in ((sl, "sl_t"), (th, "th_t"), (gs, "gs_t")):
+            vals = new([P, PACK], F32, name)
+            nc.gpsimd.dma_start(vals[:], src.rearrange("(p t) o -> p (t o)", t=PACK))
+            row_vals.append(vals)
+        sl_t, th_t, gs_t = row_vals
+
+        sc_picked = new([P, H + S], U8, "sc_picked")
+        nc.vector.tensor_copy(sc_picked[:, H:], x_sc_win[:].indirect(offs_l[:]))
+        nc.vector.tensor_copy(sc_picked[:, :H], d_sc_win[:].indirect(k1_l[:]))
+        place_scale_rows((nc.scalar,), sc_picked, sc_placed)
+        d_picked = new([P, H], U32, "d_picked", over="d_sc_win")
+        nc.vector.tensor_copy(d_picked[:], d_win[:].indirect(k1_l[:]))
+        xq = new([P, S], U32, "xq")
+        nc.vector.tensor_copy(xq[:], x_win[:].indirect(offs_l[:]))
+
+        h = []
+        for t in tiles:
+            w_t = deal(d_picked, U32, t, "d_dealt%d" % t)
+            sc_t = deal(sc_placed, U8, t, "d_sc_dealt%d" % t)
+            acc = psum.tile([P, S], F32, name="bank%d" % t)
+            nc.tensor.matmul_mx(
+                out=acc[:], lhsT=w_t[:].bitcast(FP8X4), lhsT_scale=sc_t[:],
+                rhs=xq[:].bitcast(FP8X4), rhs_scale=sc_placed[:, H:], start=True, stop=True,
+            )
+            h_t = new([P, S], F32, "h%d" % t)
+            nc.vector.tensor_scalar_mul(h_t[:], acc[:], 0.0625)
+            h.append(h_t)
+
+        bias_t = new([P, PACK], F32, "bias_t")
+        nc.vector.scalar_tensor_tensor(bias_t[:], sl_t[:], -1.0, th_t[:], ALU.mult, ALU.mult)
+
+        ds = [new([P, S], F32, "ds%d" % t) for t in tiles]
+        for pair in (0, 2):
+            for half in halves:
+                for t in (pair, pair + 1):
+                    nc.scalar.activation(ds[t][:].indirect(n1_l[:, entries(half)]), h[t][:, cols(half)], ACT.Copy)
+
+        c_sc_picked = new([P, C], U8, "c_sc_picked", over="d_sc_dealt3")
+        nc.vector.tensor_copy(c_sc_picked[:], x_sc_win[:].indirect(cand_l[:]))
+        place_scale_rows((nc.sync,), c_sc_picked, c_sc_placed)
+        c_picked = new([P, C], U32, "c_picked", over="d_dealt3")
+        nc.vector.tensor_copy(c_picked[:], x_win[:].indirect(cand_l[:]))
+        c_dealt = [deal(c_picked, U32, t, "c_dealt%d" % t) for t in tiles]
+        c_sc_dealt = [deal(c_sc_placed, U8, t, "c_sc_dealt%d" % t) for t in tiles]
+
+        s = [new([P, S], F32, "s%d" % t) for t in tiles]
+        for half in halves:
+            z = new([P, PACK, HALF], BF16, "z%d" % half)
+            for t in tiles:
+                sg = new([P, HALF], F32, "sg%d_%d" % (half, t))
+                nc.scalar.activation(
+                    sg[:], ds[t][:].indirect(n2_l[:, entries(half)]), ACT.Sigmoid,
+                    scale=sl_t[:, t : t + 1], bias=bias_t[:, t : t + 1],
+                )
+                nc.vector.scalar_tensor_tensor(
+                    z[:, t, :], h[t][:, cols(half)], gs_t[:, t : t + 1], sg[:], ALU.mult, ALU.mult
+                )
+            z_grouped = new([P, HALF, PACK], BF16, "z_grouped%d" % half)
+            nc.vector.tensor_copy(z_grouped[:], z[:].rearrange("p t c -> p c t"))
+            zq = new([P, HALF], U32, "zq%d" % half)
+            zq_sc = new([P, HALF], U8, "zq_sc%d" % half)
+            nc.vector.quantize_mx(
+                out=zq[:].bitcast(FP8X4), scales=zq_sc[:], in_=z_grouped[:].rearrange("p c t -> p (c t)")
+            )
+            for t in tiles:
+                acc = psum.tile([P, HALF], F32, name="bank%d" % (t + PACK * (1 - half)))
+                nc.tensor.matmul_mx(
+                    out=acc[:], lhsT=c_dealt[t][:].bitcast(FP8X4), lhsT_scale=c_sc_dealt[t][:],
+                    rhs=zq[:].bitcast(FP8X4), rhs_scale=zq_sc[:], start=True, stop=True,
+                )
+                nc.vector.tensor_scalar_mul(s[t][:, cols(half)], acc[:], 0.0625)
+
+        pb, rb = [], []
+        for t in tiles:
+            pb_t = new([P, W], F32, "pb%d" % t)
+            nc.scalar.activation(pb_t[:], s[t][:].indirect(n4_l[:]), ACT.Copy)
+            pa_t = new([P, W], F32, "pa%d" % t)
+            nc.scalar.activation(pa_t[:], s[t][:].indirect(n3_l[:]), ACT.Copy)
+            rb_t = new([P, W], F32, "rb%d" % t)
+            nc.vector.tensor_tensor(rb_t[:], pa_t[:], pb_t[:], ALU.subtract)
+            pb.append(pb_t)
+            rb.append(rb_t)
+        dt = [new([P, S], F32, "dt%d" % t) for t in tiles]
+        for t in tiles:
+            nc.scalar.activation(dt[t][:].indirect(n3_l[:]), pb[t][:], ACT.Copy)
+        for t in tiles:
+            nc.scalar.activation(dt[t][:].indirect(n4_l[:]), rb[t][:], ACT.Copy)
+
+        out_rows = out_0.rearrange("(p t) c -> p t c", t=PACK)
+        out_words = out_1[0].rearrange("p c t -> p (c t)").bitcast(I32)
+        yq_sc = new([P, S], U8, "yq_sc")
+        for half in halves:
+            y = new([P, PACK, HALF], F32, "y%d" % half)
+            for t in tiles:
+                far = new([P, HALF], F32, "far%d_%d" % (half, t))
+                nc.scalar.activation(far[:], dt[t][:].indirect(n5_l[:, entries(half)]), ACT.Copy)
+                nc.vector.scalar_tensor_tensor(y[:, t, :], far[:], 0.5, dt[t][:, cols(half)], ALU.mult, ALU.max)
+            nc.sync.dma_start(out_rows[:, :, cols(half)], y[:])
+            y_grouped = new([P, HALF, PACK], BF16, "y_grouped%d" % half)
+            nc.vector.tensor_copy(y_grouped[:], y[:].rearrange("p t c -> p c t"))
+            yq = new([P, HALF], U32, "yq%d" % half)
+            nc.vector.quantize_mx(
+                out=yq[:].bitcast(FP8X4), scales=yq_sc[:, cols(half)], in_=y_grouped[:].rearrange("p c t -> p (c t)")
+            )
+            nc.sync.dma_start(out_words[:, cols(half)], yq[:].bitcast(I32))
+        for q in range(4):
+            queue = nc.scalar if q % 2 else nc.sync
+            queue.dma_start(out_2[0, 4 * q : 4 * q + 4, :].bitcast(I32), yq_sc[32 * q : 32 * q + 4, :].bitcast(I32))

@@ -34,6 +34,12 @@ def tile_picked_pqhcerlswapd_none_po_kernel(
     def entries(half):
         return slice(half * HALF // PER_COL, (half + 1) * HALF // PER_COL)
 
+    def first_spans(t):
+        return [cols(0), cols(1)] if t == 0 else [slice(0, S)]
+
+    def listed(span):
+        return slice(span.start // PER_COL, span.stop // PER_COL)
+
     with ExitStack() as ctx:
         keep = ctx.enter_context(tc.tile_pool(name="keep", bufs=1))
         psum = ctx.enter_context(tc.psum_pool(name="psum", bufs=1))
@@ -58,7 +64,7 @@ def tile_picked_pqhcerlswapd_none_po_kernel(
 
         def load_scale_rows(win, src):
             rows = src[0].bitcast(I32)
-            nc.sync.dma_start(win[:].bitcast(I32), rows.unsqueeze(1).to_broadcast([16, 8, rows.shape[1]]))
+            nc.scalar.dma_start(win[:].bitcast(I32), rows.unsqueeze(1).to_broadcast([16, 8, rows.shape[1]]))
 
         def place_scale_rows(queues, picked, placed):
             for r in range(4):
@@ -66,8 +72,8 @@ def tile_picked_pqhcerlswapd_none_po_kernel(
                     placed[r:P:32, :].bitcast(I32), picked[8 * r : P : 32, :].bitcast(I32)
                 )
 
-        def deal(src, dtype, t, name):
-            dealt = new([P, P], dtype, name)
+        def deal(src, dtype, t, name, over=None):
+            dealt = new([P, P], dtype, name, over)
             nc.vector.tensor_copy(dealt[:], src[:, :H].rearrange("p (m t) -> p t m", t=PACK)[:, t, :])
             return dealt
 
@@ -76,10 +82,15 @@ def tile_picked_pqhcerlswapd_none_po_kernel(
         sc_placed = zeroed_bytes(nc.vector, H + S, "sc_placed")
         c_sc_placed = zeroed_bytes(nc.vector, C, "c_sc_placed")
 
-        k1_l = load_list(k1, "k1_l")
-        d_win = load_words(nc.scalar, d_words, "d_win")
+        d_win = load_words(nc.gpsimd, d_words, "d_win")
+        x_win = load_words(nc.gpsimd, x_words, "x_win")
+        ds = [new([P, 2 * S], F32, "ds%d" % t) for t in tiles]
+        dt = [new([P, S + PER_COL], F32, "dt%d" % t) for t in tiles]
+        for t in tiles:
+            nc.vector.memset(ds[t][:, S:], 0.0)
+            nc.vector.memset(dt[t][:, S:], 0.0)
         offs_l = load_list(offs, "offs_l")
-        x_win = load_words(nc.scalar, x_words, "x_win")
+        k1_l = load_list(k1, "k1_l")
         load_scale_rows(x_sc_win, x_scales)
         load_scale_rows(d_sc_win, d_scales)
         n1_l = load_list(n1, "n1_l")
@@ -89,78 +100,96 @@ def tile_picked_pqhcerlswapd_none_po_kernel(
         n4_l = load_list(n4, "n4_l")
         n5_l = load_list(n5, "n5_l")
 
-        row_vals = []
-        for src, name in ((sl, "sl_t"), (th, "th_t"), (gs, "gs_t")):
-            vals = new([P, PACK], F32, name)
-            nc.gpsimd.dma_start(vals[:], src.rearrange("(p t) o -> p (t o)", t=PACK))
-            row_vals.append(vals)
-        sl_t, th_t, gs_t = row_vals
-
         sc_picked = new([P, H + S], U8, "sc_picked")
         nc.vector.tensor_copy(sc_picked[:, H:], x_sc_win[:].indirect(offs_l[:]))
         nc.vector.tensor_copy(sc_picked[:, :H], d_sc_win[:].indirect(k1_l[:]))
-        place_scale_rows((nc.scalar,), sc_picked, sc_placed)
+        place_scale_rows((nc.scalar, nc.sync), sc_picked, sc_placed)
         d_picked = new([P, H], U32, "d_picked", over="d_sc_win")
         nc.vector.tensor_copy(d_picked[:], d_win[:].indirect(k1_l[:]))
         xq = new([P, S], U32, "xq")
-        nc.vector.tensor_copy(xq[:], x_win[:].indirect(offs_l[:]))
+        for half in halves:
+            nc.vector.tensor_copy(xq[:, cols(half)], x_win[:].indirect(offs_l[:, entries(half)]))
+
+        def product(acc, weights, weights_sc, moving, moving_sc):
+            nc.tensor.matmul_mx(
+                out=acc, lhsT=weights[:].bitcast(FP8X4), lhsT_scale=weights_sc[:],
+                rhs=moving.bitcast(FP8X4), rhs_scale=moving_sc, start=True, stop=True,
+            )
+
+        xq_sc = sc_placed[:, H:]
 
         h = []
         for t in tiles:
-            w_t = deal(d_picked, U32, t, "d_dealt%d" % t)
-            sc_t = deal(sc_placed, U8, t, "d_sc_dealt%d" % t)
-            acc = psum.tile([P, S], F32, name="bank%d" % t)
-            nc.tensor.matmul_mx(
-                out=acc[:], lhsT=w_t[:].bitcast(FP8X4), lhsT_scale=sc_t[:],
-                rhs=xq[:].bitcast(FP8X4), rhs_scale=sc_placed[:, H:], start=True, stop=True,
-            )
+            w_t = deal(d_picked, U32, t, "d_dealt%d" % t, over="d_words%d" % (t % 2))
+            sc_t = deal(sc_placed, U8, t, "d_sc_dealt%d" % t, over="d_bytes%d" % (t % 2))
             h_t = new([P, S], F32, "h%d" % t)
-            nc.vector.tensor_scalar_mul(h_t[:], acc[:], 0.0625)
+            for i, span in enumerate(first_spans(t)):
+                acc = psum.tile([P, span.stop - span.start], F32, name="bank%d" % (t + PACK * i))
+                product(acc[:], w_t, sc_t, xq[:, span], xq_sc[:, span])
+                nc.vector.tensor_scalar_mul(h_t[:, span], acc[:], 0.0625)
             h.append(h_t)
+
+        row_vals = []
+        for src, name, over in ((sl, "sl_t", "d_bytes0"), (th, "th_t", "d_words0"), (gs, "gs_t", "d_win")):
+            vals = new([P, PACK], F32, name, over)
+            nc.sync.dma_start(vals[:], src.rearrange("(p t) o -> p (t o)", t=PACK))
+            row_vals.append(vals)
+        sl_t, th_t, gs_t = row_vals
 
         bias_t = new([P, PACK], F32, "bias_t")
         nc.vector.scalar_tensor_tensor(bias_t[:], sl_t[:], -1.0, th_t[:], ALU.mult, ALU.mult)
 
-        ds = [new([P, S], F32, "ds%d" % t) for t in tiles]
-        for pair in (0, 2):
-            for half in halves:
-                for t in (pair, pair + 1):
-                    nc.scalar.activation(ds[t][:].indirect(n1_l[:, entries(half)]), h[t][:, cols(half)], ACT.Copy)
-
-        c_sc_picked = new([P, C], U8, "c_sc_picked", over="d_sc_dealt3")
+        c_sc_picked = new([P, C], U8, "c_sc_picked", over="d_bytes1")
         nc.vector.tensor_copy(c_sc_picked[:], x_sc_win[:].indirect(cand_l[:]))
         place_scale_rows((nc.sync,), c_sc_picked, c_sc_placed)
-        c_picked = new([P, C], U32, "c_picked", over="d_dealt3")
+        c_picked = new([P, C], U32, "c_picked", over="d_words1")
         nc.vector.tensor_copy(c_picked[:], x_win[:].indirect(cand_l[:]))
         c_dealt = [deal(c_picked, U32, t, "c_dealt%d" % t) for t in tiles]
         c_sc_dealt = [deal(c_sc_placed, U8, t, "c_sc_dealt%d" % t) for t in tiles]
 
+        def scatter_h(t, span):
+            nc.scalar.activation(ds[t][:].indirect(n1_l[:, listed(span)]), h[t][:, span], ACT.Copy)
+
+        z = new([P, PACK - 1, S], BF16, "z")
+        z_grouped = [new([P, HALF, PACK], BF16, "z_grouped%d" % half) for half in halves]
+
+        def gate(t, span, z_out):
+            sg = new([P, span.stop - span.start], F32, "sg%d_%d" % (t, span.start))
+            nc.scalar.activation(
+                sg[:], ds[t][:].indirect(n2_l[:, listed(span)]), ACT.Sigmoid,
+                scale=sl_t[:, t : t + 1], bias=bias_t[:, t : t + 1],
+            )
+            nc.vector.scalar_tensor_tensor(z_out, h[t][:, span], gs_t[:, t : t + 1], sg[:], ALU.mult, ALU.mult)
+
+        whole = slice(0, S)
+        scatter_h(0, cols(0))
+        scatter_h(1, whole)
+        scatter_h(0, cols(1))
+        scatter_h(2, whole)
+        gate(1, whole, z[:, 1, :])
+        gate(0, whole, z[:, 0, :])
+        scatter_h(3, whole)
+        gate(2, whole, z[:, 2, :])
+        for half in halves:
+            nc.vector.tensor_copy(z_grouped[half][:, :, : PACK - 1], z[:, :, cols(half)].rearrange("p t c -> p c t"))
+        zq = [new([P, HALF], U32, "zq%d" % half) for half in halves]
+        zq_sc = [new([P, HALF], U8, "zq_sc%d" % half) for half in halves]
+        for half in halves:
+            gate(PACK - 1, cols(half), z_grouped[half][:, :, PACK - 1])
+            nc.vector.quantize_mx(
+                out=zq[half][:].bitcast(FP8X4), scales=zq_sc[half][:],
+                in_=z_grouped[half][:].rearrange("p c t -> p (c t)"),
+            )
         s = [new([P, S], F32, "s%d" % t) for t in tiles]
         for half in halves:
-            z = new([P, PACK, HALF], BF16, "z%d" % half)
-            for t in tiles:
-                sg = new([P, HALF], F32, "sg%d_%d" % (half, t))
-                nc.scalar.activation(
-                    sg[:], ds[t][:].indirect(n2_l[:, entries(half)]), ACT.Sigmoid,
-                    scale=sl_t[:, t : t + 1], bias=bias_t[:, t : t + 1],
-                )
-                nc.vector.scalar_tensor_tensor(
-                    z[:, t, :], h[t][:, cols(half)], gs_t[:, t : t + 1], sg[:], ALU.mult, ALU.mult
-                )
-            z_grouped = new([P, HALF, PACK], BF16, "z_grouped%d" % half)
-            nc.vector.tensor_copy(z_grouped[:], z[:].rearrange("p t c -> p c t"))
-            zq = new([P, HALF], U32, "zq%d" % half)
-            zq_sc = new([P, HALF], U8, "zq_sc%d" % half)
-            nc.vector.quantize_mx(
-                out=zq[:].bitcast(FP8X4), scales=zq_sc[:], in_=z_grouped[:].rearrange("p c t -> p (c t)")
-            )
-            for t in tiles:
-                acc = psum.tile([P, HALF], F32, name="bank%d" % (t + PACK * (1 - half)))
-                nc.tensor.matmul_mx(
-                    out=acc[:], lhsT=c_dealt[t][:].bitcast(FP8X4), lhsT_scale=c_sc_dealt[t][:],
-                    rhs=zq[:].bitcast(FP8X4), rhs_scale=zq_sc[:], start=True, stop=True,
-                )
-                nc.vector.tensor_scalar_mul(s[t][:, cols(half)], acc[:], 0.0625)
+            acc = psum.tile([P, HALF], F32, name="bank%d" % (PACK * half))
+            product(acc[:], c_dealt[0], c_sc_dealt[0], zq[half][:], zq_sc[half][:])
+            nc.scalar.activation(s[0][:, cols(half)], acc[:], ACT.Copy, scale=0.0625)
+        for t in range(1, PACK):
+            acc = psum.tile([P, S], F32, name="bank%d" % t)
+            for half in halves:
+                product(acc[:, cols(half)], c_dealt[t], c_sc_dealt[t], zq[half][:], zq_sc[half][:])
+            nc.vector.tensor_scalar_mul(s[t][:], acc[:], 0.0625)
 
         pb, rb = [], []
         for t in tiles:
@@ -172,7 +201,6 @@ def tile_picked_pqhcerlswapd_none_po_kernel(
             nc.vector.tensor_tensor(rb_t[:], pa_t[:], pb_t[:], ALU.subtract)
             pb.append(pb_t)
             rb.append(rb_t)
-        dt = [new([P, S], F32, "dt%d" % t) for t in tiles]
         for t in tiles:
             nc.scalar.activation(dt[t][:].indirect(n3_l[:]), pb[t][:], ACT.Copy)
         for t in tiles:
@@ -181,20 +209,32 @@ def tile_picked_pqhcerlswapd_none_po_kernel(
         out_rows = out_0.rearrange("(p t) c -> p t c", t=PACK)
         out_words = out_1[0].rearrange("p c t -> p (c t)").bitcast(I32)
         yq_sc = new([P, S], U8, "yq_sc")
+        y_first = new([P, PACK - 1, S], F32, "y_first")
+        y_last = new([P, S], F32, "y_last")
+        y_grouped = [new([P, HALF, PACK], BF16, "y_grouped%d" % half) for half in halves]
+
+        def larger(t, span, y_out):
+            far = new([P, span.stop - span.start], F32, "far%d_%d" % (t, span.start))
+            nc.scalar.activation(far[:], dt[t][:].indirect(n5_l[:, listed(span)]), ACT.Copy)
+            nc.vector.scalar_tensor_tensor(y_out, far[:], 0.5, dt[t][:, span], ALU.mult, ALU.max)
+
+        for t in range(PACK - 1):
+            larger(t, whole, y_first[:, t, :])
+            nc.sync.dma_start(out_rows[:, t, :], y_first[:, t, :])
         for half in halves:
-            y = new([P, PACK, HALF], F32, "y%d" % half)
-            for t in tiles:
-                far = new([P, HALF], F32, "far%d_%d" % (half, t))
-                nc.scalar.activation(far[:], dt[t][:].indirect(n5_l[:, entries(half)]), ACT.Copy)
-                nc.vector.scalar_tensor_tensor(y[:, t, :], far[:], 0.5, dt[t][:, cols(half)], ALU.mult, ALU.max)
-            nc.sync.dma_start(out_rows[:, :, cols(half)], y[:])
-            y_grouped = new([P, HALF, PACK], BF16, "y_grouped%d" % half)
-            nc.vector.tensor_copy(y_grouped[:], y[:].rearrange("p t c -> p c t"))
+            nc.vector.tensor_copy(
+                y_grouped[half][:, :, : PACK - 1], y_first[:, :, cols(half)].rearrange("p t c -> p c t")
+            )
+        for half in halves:
+            larger(PACK - 1, cols(half), y_last[:, cols(half)])
+            nc.vector.tensor_copy(y_grouped[half][:, :, PACK - 1], y_last[:, cols(half)])
             yq = new([P, HALF], U32, "yq%d" % half)
             nc.vector.quantize_mx(
-                out=yq[:].bitcast(FP8X4), scales=yq_sc[:, cols(half)], in_=y_grouped[:].rearrange("p c t -> p (c t)")
+                out=yq[:].bitcast(FP8X4), scales=yq_sc[:, cols(half)],
+                in_=y_grouped[half][:].rearrange("p c t -> p (c t)"),
             )
             nc.sync.dma_start(out_words[:, cols(half)], yq[:].bitcast(I32))
+        nc.scalar.dma_start(out_rows[:, PACK - 1, :], y_last[:])
         for q in range(4):
             queue = nc.scalar if q % 2 else nc.sync
             queue.dma_start(out_2[0, 4 * q : 4 * q + 4, :].bitcast(I32), yq_sc[32 * q : 32 * q + 4, :].bitcast(I32))

@@ -31,17 +31,12 @@ def tile_picked_pqhcerlswapd_none_po_kernel(
     def cols(half):
         return slice(half * HALF, (half + 1) * HALF)
 
-    def entries(half):
-        return slice(half * HALF // PER_COL, (half + 1) * HALF // PER_COL)
-
-    def first_spans(t):
-        return [cols(0), cols(1)] if t == 0 else [slice(0, S)]
-
     def listed(span):
         return slice(span.start // PER_COL, span.stop // PER_COL)
 
     with ExitStack() as ctx:
         keep = ctx.enter_context(tc.tile_pool(name="keep", bufs=1))
+        reused = ctx.enter_context(tc.tile_pool(name="reused", bufs=1))
         psum = ctx.enter_context(tc.psum_pool(name="psum", bufs=1))
 
         def new(shape, dtype, name, over=None):
@@ -57,10 +52,8 @@ def tile_picked_pqhcerlswapd_none_po_kernel(
             engine.memset(plane[:].bitcast(I32), 0)
             return plane
 
-        def load_words(queue, src, name):
-            words = new([P, src.shape[2]], U32, name)
-            queue.dma_start(words[:].bitcast(I32), src[0].rearrange("p n t -> p (n t)").bitcast(I32))
-            return words
+        def load_words(words, src):
+            nc.gpsimd.dma_start(words[:].bitcast(I32), src[0].rearrange("p n t -> p (n t)").bitcast(I32))
 
         def load_scale_rows(win, src):
             rows = src[0].bitcast(I32)
@@ -82,13 +75,19 @@ def tile_picked_pqhcerlswapd_none_po_kernel(
         sc_placed = zeroed_bytes(nc.vector, H + S, "sc_placed")
         c_sc_placed = zeroed_bytes(nc.vector, C, "c_sc_placed")
 
-        d_win = load_words(nc.gpsimd, d_words, "d_win")
-        x_win = load_words(nc.gpsimd, x_words, "x_win")
+        d_win = reused.tile([P, G], U32, name="d_win", offset=0)
+        x_win = new([P, T], U32, "x_win")
+        load_words(d_win, d_words)
+        load_words(x_win, x_words)
         ds = [new([P, 2 * S], F32, "ds%d" % t) for t in tiles]
-        dt = [new([P, S + PER_COL], F32, "dt%d" % t) for t in tiles]
-        for t in tiles:
-            nc.vector.memset(ds[t][:, S:], 0.0)
-            nc.vector.memset(dt[t][:, S:], 0.0)
+        dt = [new([P, S + PER_COL], F32, "dt%d" % t) for t in range(2)]
+        for win in ds + dt:
+            nc.vector.memset(win[:, S:], 0.0)
+        dt = dt + [new([P, S], F32, "dt%d" % t) for t in range(2, PACK)]
+        warm_in = new([P, 1], F32, "warm_in")
+        warm_out = new([P, 1], F32, "warm_out")
+        nc.vector.memset(warm_in[:], 0.0)
+        nc.scalar.activation(warm_out[:], warm_in[:], ACT.Sigmoid)
         offs_l = load_list(offs, "offs_l")
         k1_l = load_list(k1, "k1_l")
         load_scale_rows(x_sc_win, x_scales)
@@ -106,10 +105,6 @@ def tile_picked_pqhcerlswapd_none_po_kernel(
         place_scale_rows((nc.scalar, nc.sync), sc_picked, sc_placed)
         d_picked = new([P, H], U32, "d_picked", over="d_sc_win")
         nc.vector.tensor_copy(d_picked[:], d_win[:].indirect(k1_l[:]))
-        xq = new([P, S], U32, "xq")
-        for half in halves:
-            nc.vector.tensor_copy(xq[:, cols(half)], x_win[:].indirect(offs_l[:, entries(half)]))
-
         def product(acc, weights, weights_sc, moving, moving_sc):
             nc.tensor.matmul_mx(
                 out=acc, lhsT=weights[:].bitcast(FP8X4), lhsT_scale=weights_sc[:],
@@ -118,20 +113,35 @@ def tile_picked_pqhcerlswapd_none_po_kernel(
 
         xq_sc = sc_placed[:, H:]
 
-        h = []
-        for t in tiles:
-            w_t = deal(d_picked, U32, t, "d_dealt%d" % t, over="d_words%d" % (t % 2))
-            sc_t = deal(sc_placed, U8, t, "d_sc_dealt%d" % t, over="d_bytes%d" % (t % 2))
-            h_t = new([P, S], F32, "h%d" % t)
-            for i, span in enumerate(first_spans(t)):
-                acc = psum.tile([P, span.stop - span.start], F32, name="bank%d" % (t + PACK * i))
-                product(acc[:], w_t, sc_t, xq[:, span], xq_sc[:, span])
-                nc.vector.tensor_scalar_mul(h_t[:, span], acc[:], 0.0625)
-            h.append(h_t)
+        xq = new([P, S], U32, "xq")
+        h = [new([P, S], F32, "h%d" % t) for t in tiles]
+        d_dealt, d_sc_dealt = {}, {}
+
+        def deal_d(t):
+            d_dealt[t] = deal(d_picked, U32, t, "d_dealt%d" % t, over="d_words%d" % (t % 2))
+            d_sc_dealt[t] = deal(sc_placed, U8, t, "d_sc_dealt%d" % t, over="d_bytes%d" % (t % 2))
+
+        def first_product(t, span, bank):
+            acc = psum.tile([P, span.stop - span.start], F32, name="bank%d" % bank)
+            product(acc[:], d_dealt[t], d_sc_dealt[t], xq[:, span], xq_sc[:, span])
+            return acc
+
+        whole = slice(0, S)
+        for half in halves:
+            nc.vector.tensor_copy(xq[:, cols(half)], x_win[:].indirect(offs_l[:, listed(cols(half))]))
+            for t in range(2):
+                if half == 0:
+                    deal_d(t)
+                acc = first_product(t, cols(half), t + PACK * half)
+                nc.vector.tensor_scalar_mul(h[t][:, cols(half)], acc[:], 0.0625)
+        for t in range(2, PACK):
+            deal_d(t)
+            acc = first_product(t, whole, t)
+            nc.vector.tensor_scalar_mul(h[t][:], acc[:], 0.0625)
 
         row_vals = []
-        for src, name, over in ((sl, "sl_t", "d_bytes0"), (th, "th_t", "d_words0"), (gs, "gs_t", "d_win")):
-            vals = new([P, PACK], F32, name, over)
+        for i, (src, name) in enumerate(((sl, "sl_t"), (th, "th_t"), (gs, "gs_t"))):
+            vals = reused.tile([P, PACK], F32, name=name, offset=32 * i)
             nc.sync.dma_start(vals[:], src.rearrange("(p t) o -> p (t o)", t=PACK))
             row_vals.append(vals)
         sl_t, th_t, gs_t = row_vals
@@ -150,32 +160,39 @@ def tile_picked_pqhcerlswapd_none_po_kernel(
         def scatter_h(t, span):
             nc.scalar.activation(ds[t][:].indirect(n1_l[:, listed(span)]), h[t][:, span], ACT.Copy)
 
-        z = new([P, PACK - 1, S], BF16, "z")
-        z_grouped = [new([P, HALF, PACK], BF16, "z_grouped%d" % half) for half in halves]
-
-        def gate(t, span, z_out):
-            sg = new([P, span.stop - span.start], F32, "sg%d_%d" % (t, span.start))
+        def gate(t, span, sg):
             nc.scalar.activation(
-                sg[:], ds[t][:].indirect(n2_l[:, listed(span)]), ACT.Sigmoid,
+                sg, ds[t][:].indirect(n2_l[:, listed(span)]), ACT.Sigmoid,
                 scale=sl_t[:, t : t + 1], bias=bias_t[:, t : t + 1],
             )
-            nc.vector.scalar_tensor_tensor(z_out, h[t][:, span], gs_t[:, t : t + 1], sg[:], ALU.mult, ALU.mult)
 
-        whole = slice(0, S)
-        scatter_h(0, cols(0))
-        scatter_h(1, whole)
-        scatter_h(0, cols(1))
-        scatter_h(2, whole)
-        gate(1, whole, z[:, 1, :])
-        gate(0, whole, z[:, 0, :])
-        scatter_h(3, whole)
-        gate(2, whole, z[:, 2, :])
+        z_grouped = [new([P, HALF, PACK], BF16, "z_grouped%d" % half) for half in halves]
         for half in halves:
-            nc.vector.tensor_copy(z_grouped[half][:, :, : PACK - 1], z[:, :, cols(half)].rearrange("p t c -> p c t"))
+            for t in range(2):
+                scatter_h(t, cols(half))
+        z_first = new([P, 2, S], BF16, "z_first")
+        for t in range(2):
+            sg = new([P, S], F32, "sg%d" % t)
+            gate(t, whole, sg[:])
+            nc.vector.scalar_tensor_tensor(z_first[:, t, :], h[t][:], gs_t[:, t : t + 1], sg[:], ALU.mult, ALU.mult)
+        for half in halves:
+            nc.vector.tensor_copy(z_grouped[half][:, :, :2], z_first[:, :, cols(half)].rearrange("p t c -> p c t"))
+        weighted = new([P, 2, S], F32, "weighted")
+        for t in range(2, PACK):
+            scatter_h(t, whole)
+            nc.vector.tensor_scalar_mul(weighted[:, t - 2, :], h[t][:], gs_t[:, t : t + 1])
+        weighted_pairs = new([P, S, 2], F32, "weighted_pairs")
+        nc.vector.tensor_copy(weighted_pairs[:], weighted[:].rearrange("p t c -> p c t"))
         zq = [new([P, HALF], U32, "zq%d" % half) for half in halves]
         zq_sc = [new([P, HALF], U8, "zq_sc%d" % half) for half in halves]
         for half in halves:
-            gate(PACK - 1, cols(half), z_grouped[half][:, :, PACK - 1])
+            sg_last = new([P, 2, HALF], F32, "sg_last%d" % half)
+            for t in range(2, PACK):
+                gate(t, cols(half), sg_last[:, t - 2, :])
+            nc.vector.tensor_tensor(
+                z_grouped[half][:, :, 2:], weighted_pairs[:, cols(half), :],
+                sg_last[:].rearrange("p t c -> p c t"), ALU.mult,
+            )
             nc.vector.quantize_mx(
                 out=zq[half][:].bitcast(FP8X4), scales=zq_sc[half][:],
                 in_=z_grouped[half][:].rearrange("p c t -> p (c t)"),
@@ -201,16 +218,18 @@ def tile_picked_pqhcerlswapd_none_po_kernel(
             nc.vector.tensor_tensor(rb_t[:], pa_t[:], pb_t[:], ALU.subtract)
             pb.append(pb_t)
             rb.append(rb_t)
-        for t in tiles:
+
+        def put_pb(t):
             nc.scalar.activation(dt[t][:].indirect(n3_l[:]), pb[t][:], ACT.Copy)
-        for t in tiles:
+
+        def put_rb(t):
             nc.scalar.activation(dt[t][:].indirect(n4_l[:]), rb[t][:], ACT.Copy)
 
         out_rows = out_0.rearrange("(p t) c -> p t c", t=PACK)
         out_words = out_1[0].rearrange("p c t -> p (c t)").bitcast(I32)
         yq_sc = new([P, S], U8, "yq_sc")
-        y_first = new([P, PACK - 1, S], F32, "y_first")
-        y_last = new([P, S], F32, "y_last")
+        y_first = new([P, 2, S], F32, "y_first")
+        y_last = [new([P, 2, HALF], F32, "y_last%d" % half) for half in halves]
         y_grouped = [new([P, HALF, PACK], BF16, "y_grouped%d" % half) for half in halves]
 
         def larger(t, span, y_out):
@@ -218,23 +237,29 @@ def tile_picked_pqhcerlswapd_none_po_kernel(
             nc.scalar.activation(far[:], dt[t][:].indirect(n5_l[:, listed(span)]), ACT.Copy)
             nc.vector.scalar_tensor_tensor(y_out, far[:], 0.5, dt[t][:, span], ALU.mult, ALU.max)
 
-        for t in range(PACK - 1):
-            larger(t, whole, y_first[:, t, :])
-            nc.sync.dma_start(out_rows[:, t, :], y_first[:, t, :])
+        for t in tiles:
+            put_pb(t)
+        put_rb(0)
+        put_rb(1)
+        larger(0, whole, y_first[:, 0, :])
+        put_rb(2)
+        larger(1, whole, y_first[:, 1, :])
+        nc.sync.dma_start(out_rows[:, :2, :], y_first[:])
         for half in halves:
-            nc.vector.tensor_copy(
-                y_grouped[half][:, :, : PACK - 1], y_first[:, :, cols(half)].rearrange("p t c -> p c t")
-            )
+            nc.vector.tensor_copy(y_grouped[half][:, :, :2], y_first[:, :, cols(half)].rearrange("p t c -> p c t"))
+        larger(2, cols(0), y_last[0][:, 0, :])
+        put_rb(3)
+        larger(2, cols(1), y_last[1][:, 0, :])
         for half in halves:
-            larger(PACK - 1, cols(half), y_last[:, cols(half)])
-            nc.vector.tensor_copy(y_grouped[half][:, :, PACK - 1], y_last[:, cols(half)])
+            larger(3, cols(half), y_last[half][:, 1, :])
+            nc.vector.tensor_copy(y_grouped[half][:, :, 2:], y_last[half][:].rearrange("p t c -> p c t"))
+            nc.sync.dma_start(out_rows[:, 2:, cols(half)], y_last[half][:])
             yq = new([P, HALF], U32, "yq%d" % half)
             nc.vector.quantize_mx(
                 out=yq[:].bitcast(FP8X4), scales=yq_sc[:, cols(half)],
                 in_=y_grouped[half][:].rearrange("p c t -> p (c t)"),
             )
             nc.sync.dma_start(out_words[:, cols(half)], yq[:].bitcast(I32))
-        nc.scalar.dma_start(out_rows[:, PACK - 1, :], y_last[:])
         for q in range(4):
             queue = nc.scalar if q % 2 else nc.sync
             queue.dma_start(out_2[0, 4 * q : 4 * q + 4, :].bitcast(I32), yq_sc[32 * q : 32 * q + 4, :].bitcast(I32))

@@ -72,15 +72,15 @@ def tile_picked_pqhcerlswapd_none_po_kernel(
 
         d_sc_win = new([P, G], U8, "d_sc_win")
         x_sc_win = new([P, T], U8, "x_sc_win")
-        sc_placed = zeroed_bytes(nc.vector, H + S, "sc_placed")
-        c_sc_placed = zeroed_bytes(nc.vector, C, "c_sc_placed")
 
         d_win = reused.tile([P, G], U32, name="d_win", offset=0)
         x_win = new([P, T], U32, "x_win")
         load_words(d_win, d_words)
         load_words(x_win, x_words)
-        ds = [new([P, 2 * S], F32, "ds%d" % t) for t in tiles]
-        dt = [new([P, S + PER_COL], F32, "dt%d" % t) for t in range(2)]
+        sc_placed = zeroed_bytes(nc.gpsimd, H + S, "sc_placed")
+        c_sc_placed = zeroed_bytes(nc.gpsimd, C, "c_sc_placed")
+        ds = [new([P, 513 if t < 2 else 353], F32, "ds%d" % t) for t in tiles]
+        dt = [new([P, S + PER_COL + 1], F32, "dt%d" % t) for t in range(2)]
         for win in ds + dt:
             nc.vector.memset(win[:, S:], 0.0)
         dt = dt + [new([P, S], F32, "dt%d" % t) for t in range(2, PACK)]

from contextlib import ExitStack

import concourse.mybir as mybir

K, T, S, G, H, C, W = 512, 1024, 256, 2048, 512, 512, 128
FLOPS = 2 * K * H * S + 2 * K * C * S

F32 = mybir.dt.float32
BF16 = mybir.dt.bfloat16
I32 = mybir.dt.int32
U32 = mybir.dt.uint32
U16 = mybir.dt.uint16
U8 = mybir.dt.uint8
FP8X4 = mybir.dt.float8_e4m3fn_x4
ACT = mybir.ActivationFunctionType
ALU = mybir.AluOpType

P = 128
PACK = 4
HALF = S // 2
PER_COL = 16


def tile_picked_pqhcerlswapd_none_po_kernel(
    tc, x_words, x_scales, d_words, d_scales, sl, th, gs, offs, k1, n1, n2, cand, n3, n4, n5, out_0, out_1, out_2
):
    nc = tc.nc
    tiles = range(PACK)
    halves = range(2)

    def cols(half):
        return slice(half * HALF, (half + 1) * HALF)

    def listed(span):
        return slice(span.start // PER_COL, span.stop // PER_COL)

    with ExitStack() as ctx:
        keep = ctx.enter_context(tc.tile_pool(name="keep", bufs=1))
        reused = ctx.enter_context(tc.tile_pool(name="reused", bufs=1))
        psum = ctx.enter_context(tc.psum_pool(name="psum", bufs=1))

        def new(shape, dtype, name, over=None):
            return keep.tile(shape, dtype, name=name, tag=over or name, align_bytes=64)

        def load_list(src, name):
            lst = new(list(src.shape), U16, name)
            nc.sync.dma_start(lst[:], src)
            return lst

        def zeroed_bytes(engine, width, name):
            plane = new([P, width], U8, name)
            engine.memset(plane[:].bitcast(I32), 0)
            return plane

        def load_words(words, src):
            nc.gpsimd.dma_start(words[:].bitcast(I32), src[0].rearrange("p n t -> p (n t)").bitcast(I32))

        def load_scale_rows(win, src):
            rows = src[0].bitcast(I32)
            nc.scalar.dma_start(win[:].bitcast(I32), rows.unsqueeze(1).to_broadcast([16, 8, rows.shape[1]]))

        def place_scale_rows(queues, picked, placed):
            for r in range(4):
                queues[r % len(queues)].dma_start(
                    placed[r:P:32, :].bitcast(I32), picked[8 * r : P : 32, :].bitcast(I32)
                )

        def deal(src, dtype, t, name, over=None):
            dealt = new([P, P], dtype, name, over)
            nc.vector.tensor_copy(dealt[:], src[:, :H].rearrange("p (m t) -> p t m", t=PACK)[:, t, :])
            return dealt

        d_sc_win = new([P, G], U8, "d_sc_win")
        x_sc_win = new([P, T], U8, "x_sc_win")

        d_win = reused.tile([P, G], U32, name="d_win", offset=0)
        x_win = new([P, T], U32, "x_win")
        load_words(d_win, d_words)
        load_words(x_win, x_words)
        sc_placed = zeroed_bytes(nc.gpsimd, H + S, "sc_placed")
        c_sc_placed = zeroed_bytes(nc.gpsimd, C, "c_sc_placed")
        ds = [new([P, 513 if t < 2 else 353], F32, "ds%d" % t) for t in tiles]
        dt = [new([P, S + PER_COL + 1], F32, "dt%d" % t) for t in range(2)]
        for win in ds + dt:
            nc.vector.memset(win[:, S:], 0.0)
        dt = dt + [new([P, S], F32, "dt%d" % t) for t in range(2, PACK)]
        warm_in = new([P, 1], F32, "warm_in")
        warm_out = new([P, 1], F32, "warm_out")
        nc.vector.memset(warm_in[:], 0.0)
        nc.scalar.activation(warm_out[:], warm_in[:], ACT.Sigmoid)
        offs_l = load_list(offs, "offs_l")
        k1_l = load_list(k1, "k1_l")
        load_scale_rows(x_sc_win, x_scales)
        load_scale_rows(d_sc_win, d_scales)
        n1_l = load_list(n1, "n1_l")
        n2_l = load_list(n2, "n2_l")
        cand_l = load_list(cand, "cand_l")
        n3_l = load_list(n3, "n3_l")
        n4_l = load_list(n4, "n4_l")
        n5_l = load_list(n5, "n5_l")

        sc_picked = new([P, H + S], U8, "sc_picked")
        nc.vector.tensor_copy(sc_picked[:, H:], x_sc_win[:].indirect(offs_l[:]))
        nc.vector.tensor_copy(sc_picked[:, :H], d_sc_win[:].indirect(k1_l[:]))
        place_scale_rows((nc.scalar, nc.sync), sc_picked, sc_placed)
        d_picked = new([P, H], U32, "d_picked", over="d_sc_win")
        nc.vector.tensor_copy(d_picked[:], d_win[:].indirect(k1_l[:]))
        def product(acc, weights, weights_sc, moving, moving_sc):
            nc.tensor.matmul_mx(
                out=acc, lhsT=weights[:].bitcast(FP8X4), lhsT_scale=weights_sc[:],
                rhs=moving.bitcast(FP8X4), rhs_scale=moving_sc, start=True, stop=True,
            )

        xq_sc = sc_placed[:, H:]

        xq = new([P, S], U32, "xq")
        h = [new([P, S], F32, "h%d" % t) for t in tiles]
        d_dealt, d_sc_dealt = {}, {}

        def deal_d(t):
            d_dealt[t] = deal(d_picked, U32, t, "d_dealt%d" % t, over="d_words%d" % (t % 2))
            d_sc_dealt[t] = deal(sc_placed, U8, t, "d_sc_dealt%d" % t, over="d_bytes%d" % (t % 2))

        def first_product(t, span, bank):
            acc = psum.tile([P, span.stop - span.start], F32, name="bank%d" % bank)
            product(acc[:], d_dealt[t], d_sc_dealt[t], xq[:, span], xq_sc[:, span])
            return acc

        whole = slice(0, S)
        for half in halves:
            nc.vector.tensor_copy(xq[:, cols(half)], x_win[:].indirect(offs_l[:, listed(cols(half))]))
            for t in range(2):
                if half == 0:
                    deal_d(t)
                acc = first_product(t, cols(half), t + PACK * half)
                nc.vector.tensor_scalar_mul(h[t][:, cols(half)], acc[:], 0.0625)
        for t in range(2, PACK):
            deal_d(t)
            acc = first_product(t, whole, t)
            nc.vector.tensor_scalar_mul(h[t][:], acc[:], 0.0625)

        row_vals = []
        for i, (src, name) in enumerate(((sl, "sl_t"), (th, "th_t"), (gs, "gs_t"))):
            vals = reused.tile([P, PACK], F32, name=name, offset=32 * i)
            nc.sync.dma_start(vals[:], src.rearrange("(p t) o -> p (t o)", t=PACK))
            row_vals.append(vals)
        sl_t, th_t, gs_t = row_vals

        bias_t = new([P, PACK], F32, "bias_t")
        nc.vector.scalar_tensor_tensor(bias_t[:], sl_t[:], -1.0, th_t[:], ALU.mult, ALU.mult)

        c_sc_picked = new([P, C], U8, "c_sc_picked", over="d_bytes1")
        nc.vector.tensor_copy(c_sc_picked[:], x_sc_win[:].indirect(cand_l[:]))
        place_scale_rows((nc.sync,), c_sc_picked, c_sc_placed)
        c_picked = new([P, C], U32, "c_picked", over="d_words1")
        nc.vector.tensor_copy(c_picked[:], x_win[:].indirect(cand_l[:]))
        c_dealt = [deal(c_picked, U32, t, "c_dealt%d" % t) for t in tiles]
        c_sc_dealt = [deal(c_sc_placed, U8, t, "c_sc_dealt%d" % t) for t in tiles]

        def scatter_h(t, span):
            nc.scalar.activation(ds[t][:].indirect(n1_l[:, listed(span)]), h[t][:, span], ACT.Copy)

        def gate(t, span, sg):
            nc.scalar.activation(
                sg, ds[t][:].indirect(n2_l[:, listed(span)]), ACT.Sigmoid,
                scale=sl_t[:, t : t + 1], bias=bias_t[:, t : t + 1],
            )

        z_grouped = [new([P, HALF, PACK], BF16, "z_grouped%d" % half) for half in halves]
        for half in halves:
            for t in range(2):
                scatter_h(t, cols(half))
        z_first = new([P, 2, S], BF16, "z_first")
        for t in range(2):
            sg = new([P, S], F32, "sg%d" % t)
            gate(t, whole, sg[:])
            nc.vector.scalar_tensor_tensor(z_first[:, t, :], h[t][:], gs_t[:, t : t + 1], sg[:], ALU.mult, ALU.mult)
        for half in halves:
            nc.vector.tensor_copy(z_grouped[half][:, :, :2], z_first[:, :, cols(half)].rearrange("p t c -> p c t"))
        weighted = new([P, 2, S], F32, "weighted")
        for t in range(2, PACK):
            scatter_h(t, whole)
            nc.vector.tensor_scalar_mul(weighted[:, t - 2, :], h[t][:], gs_t[:, t : t + 1])
        weighted_pairs = new([P, S, 2], F32, "weighted_pairs")
        nc.vector.tensor_copy(weighted_pairs[:], weighted[:].rearrange("p t c -> p c t"))
        zq = [new([P, HALF], U32, "zq%d" % half) for half in halves]
        zq_sc = [new([P, HALF], U8, "zq_sc%d" % half) for half in halves]
        for half in halves:
            sg_last = new([P, 2, HALF], F32, "sg_last%d" % half)
            for t in range(2, PACK):
                gate(t, cols(half), sg_last[:, t - 2, :])
            nc.vector.tensor_tensor(
                z_grouped[half][:, :, 2:], weighted_pairs[:, cols(half), :],
                sg_last[:].rearrange("p t c -> p c t"), ALU.mult,
            )
            nc.vector.quantize_mx(
                out=zq[half][:].bitcast(FP8X4), scales=zq_sc[half][:],
                in_=z_grouped[half][:].rearrange("p c t -> p (c t)"),
            )
        s = [new([P, S], F32, "s%d" % t) for t in tiles]
        for half in halves:
            acc = psum.tile([P, HALF], F32, name="bank%d" % (PACK * half))
            product(acc[:], c_dealt[0], c_sc_dealt[0], zq[half][:], zq_sc[half][:])
            nc.scalar.activation(s[0][:, cols(half)], acc[:], ACT.Copy, scale=0.0625)
        for t in range(1, PACK):
            acc = psum.tile([P, S], F32, name="bank%d" % t)
            for half in halves:
                product(acc[:, cols(half)], c_dealt[t], c_sc_dealt[t], zq[half][:], zq_sc[half][:])
            nc.vector.tensor_scalar_mul(s[t][:], acc[:], 0.0625)

        pb, rb = [], []
        for t in tiles:
            pb_t = new([P, W], F32, "pb%d" % t)
            nc.scalar.activation(pb_t[:], s[t][:].indirect(n4_l[:]), ACT.Copy)
            pa_t = new([P, W], F32, "pa%d" % t)
            nc.scalar.activation(pa_t[:], s[t][:].indirect(n3_l[:]), ACT.Copy)
            rb_t = new([P, W], F32, "rb%d" % t)
            nc.vector.tensor_tensor(rb_t[:], pa_t[:], pb_t[:], ALU.subtract)
            pb.append(pb_t)
            rb.append(rb_t)

        def put_pb(t):
            nc.scalar.activation(dt[t][:].indirect(n3_l[:]), pb[t][:], ACT.Copy)

        def put_rb(t):
            nc.scalar.activation(dt[t][:].indirect(n4_l[:]), rb[t][:], ACT.Copy)

        out_rows = out_0.rearrange("(p t) c -> p t c", t=PACK)
        out_words = out_1[0].rearrange("p c t -> p (c t)").bitcast(I32)
        yq_sc = new([P, S], U8, "yq_sc")
        y_first = new([P, 2, S], F32, "y_first")
        y_last = [new([P, 2, HALF], F32, "y_last%d" % half) for half in halves]
        y_grouped = [new([P, HALF, PACK], BF16, "y_grouped%d" % half) for half in halves]

        def larger(t, span, y_out):
            far = new([P, span.stop - span.start], F32, "far%d_%d" % (t, span.start))
            nc.scalar.activation(far[:], dt[t][:].indirect(n5_l[:, listed(span)]), ACT.Copy)
            nc.vector.scalar_tensor_tensor(y_out, far[:], 0.5, dt[t][:, span], ALU.mult, ALU.max)

        for t in tiles:
            put_pb(t)
        put_rb(0)
        put_rb(1)
        larger(0, whole, y_first[:, 0, :])
        put_rb(2)
        larger(1, whole, y_first[:, 1, :])
        nc.sync.dma_start(out_rows[:, :2, :], y_first[:])
        for half in halves:
            nc.vector.tensor_copy(y_grouped[half][:, :, :2], y_first[:, :, cols(half)].rearrange("p t c -> p c t"))
        larger(2, cols(0), y_last[0][:, 0, :])
        put_rb(3)
        larger(2, cols(1), y_last[1][:, 0, :])
        for half in halves:
            larger(3, cols(half), y_last[half][:, 1, :])
            nc.vector.tensor_copy(y_grouped[half][:, :, 2:], y_last[half][:].rearrange("p t c -> p c t"))
            nc.sync.dma_start(out_rows[:, 2:, cols(half)], y_last[half][:])
            yq = new([P, HALF], U32, "yq%d" % half)
            nc.vector.quantize_mx(
                out=yq[:].bitcast(FP8X4), scales=yq_sc[:, cols(half)],
                in_=y_grouped[half][:].rearrange("p c t -> p (c t)"),
            )
            nc.sync.dma_start(out_words[:, cols(half)], yq[:].bitcast(I32))
        for q in range(4):
            queue = nc.scalar if q % 2 else nc.sync
            queue.dma_start(out_2[0, 4 * q : 4 * q + 4, :].bitcast(I32), yq_sc[32 * q : 32 * q + 4, :].bitcast(I32))
